import numpy as np
import ml_dtypes

BF16 = ml_dtypes.bfloat16


def bf(x):
    return np.asarray(x, np.float32).astype(BF16)


def f32(x):
    return np.asarray(x, np.float32)


def f64(x):
    return np.asarray(x).astype(np.float64)


def striped(idx):
    return np.tile(idx.reshape(-1, 16).T, (8, 1))


S, K, M, N, E, Q, V, D = 512, 128, 128, 128, 1, 128, 64, 8


def setup_inputs():
    return {"base": bf(np.random.standard_normal((M, S))), "x": bf(np.random.standard_normal((K, N))), "w": bf(1.5 * np.random.standard_normal((E, K, M)) / np.sqrt(K)), "b": f32(0.5 * np.random.standard_normal((M, 1))), "offs": striped(np.random.permutation(S)[:N])}


def reference(base, x, w, b, offs):
    idx = offs[:16].T.reshape(-1)
    z = f64(base).copy()
    for e in range(E):
        z[:, idx[e * Q : (e + 1) * Q]] += f64(w)[e].T @ f64(x)[:, e * Q : (e + 1) * Q]
    z = np.maximum(z + f64(b), 0.0)
    return z.reshape(M, V, D).mean(axis=2)

@@ -1,0 +1,45 @@
+import concourse.mybir as mybir
+from concourse.masks import make_identity
+
+BF16, F32, U16 = mybir.dt.bfloat16, mybir.dt.float32, mybir.dt.uint16
+ALU = mybir.AluOpType
+
+K, M, N, S = 128, 128, 128, 512
+POOL = 8
+
+FLOPS = 2 * K * M * N
+
+
+def tile_rows_unpool_mean_relu_kernel(tc, base, x, w, b, offs, out):
+    nc = tc.nc
+    with (
+        tc.tile_pool(name="held", bufs=1) as held,
+        tc.psum_pool(name="psum", bufs=1) as psum,
+    ):
+        base_tile = held.tile([M, S], BF16)
+        nc.sync.dma_start(base_tile[:], base)
+        w_tile = held.tile([K, M], BF16)
+        nc.sync.dma_start(w_tile[:], w.rearrange("e k m -> (e k) m"))
+        x_tile = held.tile([K, N], BF16)
+        nc.sync.dma_start(x_tile[:], x)
+        offsets = held.tile([128, N // 16], U16)
+        nc.sync.dma_start(offsets[:], offs)
+        bias = held.tile([M, 1], F32)
+        nc.scalar.dma_start(bias[:], b)
+
+        ident = held.tile([128, 128], BF16)
+        make_identity(nc, ident[:])
+
+        window = psum.tile([M, S], F32)
+        nc.tensor.matmul(window[:], ident[:], base_tile[:], start=True, stop=False)
+        nc.tensor.matmul(window[:].indirect(offsets[:]), w_tile[:], x_tile[:], start=False, stop=True)
+
+        activated = held.tile([M, S], F32)
+        nc.vector.tensor_scalar(activated[:], window[:], bias[:, 0:1], 0.0, op0=ALU.add, op1=ALU.max)
+        sums = held.tile([M, S // POOL], F32)
+        nc.vector.tensor_reduce(
+            sums[:], activated[:].rearrange("p (v d) -> p v d", d=POOL), axis=mybir.AxisListType.X, op=ALU.add
+        )
+        means = held.tile([M, S // POOL], F32)
+        nc.vector.tensor_scalar_mul(means[:], sums[:], 1.0 / POOL)
+        nc.sync.dma_start(out, means[:])

@@ -3,8 +3,10 @@ from concourse.masks import make_identity
 
 BF16, F32, U16 = mybir.dt.bfloat16, mybir.dt.float32, mybir.dt.uint16
 ALU = mybir.AluOpType
+RELU = mybir.ActivationFunctionType.Relu
 
 K, M, N, S = 128, 128, 128, 512
+HALVES = 2
 POOL = 8
 
 FLOPS = 2 * K * M * N
@@ -27,6 +29,13 @@ def tile_rows_unpool_mean_relu_kernel(tc, base, x, w, b, offs, out):
         bias = held.tile([M, 1], F32)
         nc.scalar.dma_start(bias[:], b)
 
+        early = held.tile([M, 1], F32)
+        nc.vector.memset(early[:], 0.0)
+        nc.scalar.activation(early[:], early[:], RELU)
+
+        bias_part = held.tile([M, 1], F32)
+        nc.vector.tensor_scalar_mul(bias_part[:], bias[:], 1.0 / POOL)
+
         ident = held.tile([128, 128], BF16)
         make_identity(nc, ident[:])
 
@@ -34,12 +43,13 @@ def tile_rows_unpool_mean_relu_kernel(tc, base, x, w, b, offs, out):
         nc.tensor.matmul(window[:], ident[:], base_tile[:], start=True, stop=False)
         nc.tensor.matmul(window[:].indirect(offsets[:]), w_tile[:], x_tile[:], start=False, stop=True)
 
-        activated = held.tile([M, S], F32)
-        nc.vector.tensor_scalar(activated[:], window[:], bias[:, 0:1], 0.0, op0=ALU.add, op1=ALU.max)
-        sums = held.tile([M, S // POOL], F32)
-        nc.vector.tensor_reduce(
-            sums[:], activated[:].rearrange("p (v d) -> p v d", d=POOL), axis=mybir.AxisListType.X, op=ALU.add
-        )
         means = held.tile([M, S // POOL], F32)
-        nc.vector.tensor_scalar_mul(means[:], sums[:], 1.0 / POOL)
+        for h in range(HALVES):
+            cells = slice(h * S // HALVES, (h + 1) * S // HALVES)
+            pooled = slice(cells.start // POOL, cells.stop // POOL)
+            activated = held.tile([M, S // HALVES], F32, name=f"activated{h}")
+            nc.scalar.activation(activated[:], window[:, cells], RELU, bias=bias_part[:, 0:1], scale=1.0 / POOL)
+            nc.vector.tensor_reduce(
+                means[:, pooled], activated[:].rearrange("p (v d) -> p v d", d=POOL), axis=mybir.AxisListType.X, op=ALU.add
+            )
         nc.sync.dma_start(out, means[:])

@@ -27,7 +27,7 @@ def tile_rows_unpool_mean_relu_kernel(tc, base, x, w, b, offs, out):
         offsets = held.tile([128, N // 16], U16)
         nc.sync.dma_start(offsets[:], offs)
         bias = held.tile([M, 1], F32)
-        nc.scalar.dma_start(bias[:], b)
+        nc.sync.dma_start(bias[:], b)
 
         early = held.tile([M, 1], F32)
         nc.vector.memset(early[:], 0.0)

import concourse.mybir as mybir
from concourse.masks import make_identity

BF16, F32, U16 = mybir.dt.bfloat16, mybir.dt.float32, mybir.dt.uint16
ALU = mybir.AluOpType
RELU = mybir.ActivationFunctionType.Relu

K, M, N, S = 128, 128, 128, 512
HALVES = 2
POOL = 8

FLOPS = 2 * K * M * N


def tile_rows_unpool_mean_relu_kernel(tc, base, x, w, b, offs, out):
    nc = tc.nc
    with (
        tc.tile_pool(name="held", bufs=1) as held,
        tc.psum_pool(name="psum", bufs=1) as psum,
    ):
        base_tile = held.tile([M, S], BF16)
        nc.sync.dma_start(base_tile[:], base)
        w_tile = held.tile([K, M], BF16)
        nc.sync.dma_start(w_tile[:], w.rearrange("e k m -> (e k) m"))
        x_tile = held.tile([K, N], BF16)
        nc.sync.dma_start(x_tile[:], x)
        offsets = held.tile([128, N // 16], U16)
        nc.sync.dma_start(offsets[:], offs)
        bias = held.tile([M, 1], F32)
        nc.sync.dma_start(bias[:], b)

        early = held.tile([M, 1], F32)
        nc.vector.memset(early[:], 0.0)
        nc.scalar.activation(early[:], early[:], RELU)

        bias_part = held.tile([M, 1], F32)
        nc.vector.tensor_scalar_mul(bias_part[:], bias[:], 1.0 / POOL)

        ident = held.tile([128, 128], BF16)
        make_identity(nc, ident[:])

        window = psum.tile([M, S], F32)
        nc.tensor.matmul(window[:], ident[:], base_tile[:], start=True, stop=False)
        nc.tensor.matmul(window[:].indirect(offsets[:]), w_tile[:], x_tile[:], start=False, stop=True)

        means = held.tile([M, S // POOL], F32)
        for h in range(HALVES):
            cells = slice(h * S // HALVES, (h + 1) * S // HALVES)
            pooled = slice(cells.start // POOL, cells.stop // POOL)
            activated = held.tile([M, S // HALVES], F32, name=f"activated{h}")
            nc.scalar.activation(activated[:], window[:, cells], RELU, bias=bias_part[:, 0:1], scale=1.0 / POOL)
            nc.vector.tensor_reduce(
                means[:, pooled], activated[:].rearrange("p (v d) -> p v d", d=POOL), axis=mybir.AxisListType.X, op=ALU.add
            )
        nc.sync.dma_start(out, means[:])
